import numpy as np
CORES = [1,2,9,10,17,18,25,26,33,34,41,42,49,50,57,58,65,66,73,74,81,82,89,90,97,98,105,106,113,114,121,122]
N = 32
ROOT = 19
def setup_inputs(rng):
    return {"x": rng.standard_normal((N, 128, 128), dtype=np.float32)}
def reference(x):
    y = np.full((N, 128, N * 128), np.nan, x.dtype)
    y[ROOT] = np.concatenate(list(x), axis=1)
    return {"y": y}

@@ -1,0 +1,70 @@
+SCRATCH = {
+    "land": ("sbuf", [128, 32 * 128], "float32"),
+}
+SEMAPHORES = ["loaded", "got", "sent", "st0", "st1", "st2"] + ["arr%d" % c for c in range(16)]
+
+W = 128
+DIE0_CHIPS = (2, 6, 10, 14, 3, 7, 13)
+RELAY = {0: 66, 4: 67, 12: 67, 2: 70, 6: 70, 10: 71, 14: 71}
+
+
+def rank_program(g, core, T, topo):
+    root = T.cores[T.root]
+    root_chip = topo.chip(root)
+    mate_chip = root_chip ^ 1
+    chip = topo.chip(core)
+    rank = T.rank_of(core)
+    sent = [0]
+
+    def gatherer(c):
+        if c == root_chip:
+            return root
+        return 8 * c + (6 if c in DIE0_CHIPS else 2)
+
+    def send(dst, lo, hi, sem):
+        rid, pid, _se = topo.addr(dst)
+        m = topo.mask(core, dst)
+        g.remote_dma(T.land[:, lo:hi], T.land[:, lo:hi], T.sem[sem], T.sem.sent, pid, rid, m)
+        sent[0] += bin(m).count("1")
+
+    def pair(c):
+        return 2 * W * c, 2 * W * (c + 1)
+
+    if rank is not None:
+        g.sync.dma_start(T.land[:, W * rank:W * (rank + 1)], T.x[:, :]).then_inc(T.sem.loaded, 16)
+
+    if core == root:
+        queues = (g.sync, g.scalar, g)
+        stored = [0, 0, 0]
+        for k in range(8):
+            q = k % 3
+            for c in (2 * k, 2 * k + 1):
+                queues[q].wait_ge(T.sem["arr%d" % c], 16 if c == root_chip else 8)
+                if c == root_chip:
+                    queues[q].wait_ge(T.sem.loaded, 16)
+            lo, hi = 4 * W * k, 4 * W * (k + 1)
+            queues[q].dma_start(T.y[:, lo:hi], T.land[:, lo:hi]).then_inc(T.sem["st%d" % q], 16)
+            stored[q] += 16
+        for q in range(3):
+            queues[q].wait_ge(T.sem["st%d" % q], stored[q])
+        return
+
+    gath = gatherer(chip)
+    if rank is not None:
+        g.wait_ge(T.sem.loaded, 16)
+        if core != gath:
+            send(gath, W * rank, W * (rank + 1), "arr%d" % chip if gath == root else "got")
+
+    if core == gath:
+        g.wait_ge(T.sem.got, 16 if rank is not None else 32)
+        lo, hi = pair(chip)
+        send(root if (chip & 1) or chip == mate_chip else RELAY[chip], lo, hi, "arr%d" % chip)
+
+    for c in sorted(RELAY):
+        if RELAY[c] == core:
+            g.wait_ge(T.sem["arr%d" % c], 8)
+            lo, hi = pair(c)
+            send(root, lo, hi, "arr%d" % c)
+
+    if sent[0]:
+        g.wait_ge(T.sem.sent, sent[0])

@@ -1,70 +1,101 @@
 SCRATCH = {
     "land": ("sbuf", [128, 32 * 128], "float32"),
+    "half": ("dram", [4, 128, 64], "float32"),
 }
-SEMAPHORES = ["loaded", "got", "sent", "st0", "st1", "st2"] + ["arr%d" % c for c in range(16)]
+SEMAPHORES = ["loaded", "got", "sent", "ha", "hb", "st0", "st1", "st2"] + ["arr%d" % c for c in range(16)]
 
 W = 128
-DIE0_CHIPS = (2, 6, 10, 14, 3, 7, 13)
-RELAY = {0: 66, 4: 67, 12: 67, 2: 70, 6: 70, 10: 71, 14: 71}
+ROOT = 74
+DIE0_CHIPS = (4, 5, 10, 11, 14, 15)
+RELAY = {2: 66, 6: 67, 12: 67, 4: 70, 10: 71, 14: 71}
+HALVED = {0: 0, 3: 2}
+
+
+def blocks(first, n=1):
+    return ("land", W * first, W * (first + n))
+
+
+def sends():
+    ld = ("loaded", 16)
+    s = [
+        (66, ROOT, blocks(17), "arr8", ld),
+        (65, 70, blocks(16), "got", ld),
+        (70, ROOT, blocks(16), "arr8", ("got", 16)),
+        (73, ROOT, blocks(18), "arr9", ld),
+        (1, 66, ("half", 0), "ha", ld),
+        (1, 70, ("half", 1), "ha", ld),
+        (66, ROOT, ("half", 0), "ha", ("ha", 8)),
+        (70, ROOT, ("half", 1), "ha", ("ha", 8)),
+        (2, ROOT, blocks(1), "arr0", ld),
+        (9, 14, blocks(2), "got", ld),
+        (14, ROOT, blocks(2), "arr1", ("got", 16)),
+        (10, ROOT, ("half", 2), "hb", ld),
+        (10, 14, ("half", 3), "hb", ld),
+        (14, ROOT, ("half", 3), "hb", ("hb", 16)),
+    ]
+    for c in (2, 3, 4, 5, 6, 7, 10, 11, 12, 13, 14, 15):
+        arr = "arr%d" % c
+        if c in DIE0_CHIPS:
+            gath = 8 * c + 6
+            s.append((8 * c + 1, gath, blocks(2 * c), "got", ld))
+            s.append((8 * c + 2, gath, blocks(2 * c + 1), "got", ld))
+            ready = [("got", 32)]
+        else:
+            gath = 8 * c + 2
+            s.append((8 * c + 1, gath, blocks(2 * c), "got", ld))
+            ready = [ld, ("got", 16)]
+        if c & 1:
+            s.append((gath, ROOT, blocks(2 * c, 2), arr) + tuple(ready))
+        else:
+            s.append((gath, RELAY[c], blocks(2 * c, 2), arr) + tuple(ready))
+            s.append((RELAY[c], ROOT, blocks(2 * c, 2), arr, (arr, 8)))
+    return s
 
 
 def rank_program(g, core, T, topo):
-    root = T.cores[T.root]
-    root_chip = topo.chip(root)
-    mate_chip = root_chip ^ 1
-    chip = topo.chip(core)
     rank = T.rank_of(core)
-    sent = [0]
-
-    def gatherer(c):
-        if c == root_chip:
-            return root
-        return 8 * c + (6 if c in DIE0_CHIPS else 2)
-
-    def send(dst, lo, hi, sem):
-        rid, pid, _se = topo.addr(dst)
-        m = topo.mask(core, dst)
-        g.remote_dma(T.land[:, lo:hi], T.land[:, lo:hi], T.sem[sem], T.sem.sent, pid, rid, m)
-        sent[0] += bin(m).count("1")
-
-    def pair(c):
-        return 2 * W * c, 2 * W * (c + 1)
 
     if rank is not None:
-        g.sync.dma_start(T.land[:, W * rank:W * (rank + 1)], T.x[:, :]).then_inc(T.sem.loaded, 16)
+        if rank in HALVED:
+            h = HALVED[rank]
+            g.sync.dma_start(T.half[h:h + 2], T.x[:, :]).then_inc(T.sem.loaded, 16)
+        else:
+            g.sync.dma_start(T.land[:, W * rank:W * (rank + 1)], T.x[:, :]).then_inc(T.sem.loaded, 16)
 
-    if core == root:
+    if core == ROOT:
+        stores = [
+            ([("arr8", 16), ("arr9", 16), ("loaded", 16)], 16, 4, None),
+            ([("arr0", 8), ("arr1", 8)], 1, 2, None),
+            ([("hb", 16)], 3, 1, 2),
+            ([("ha", 16)], 0, 1, 0),
+        ]
+        for k in (1, 2, 3, 5, 6, 7):
+            stores.append(([("arr%d" % (2 * k), 8), ("arr%d" % (2 * k + 1), 8)], 4 * k, 4, None))
         queues = (g.sync, g.scalar, g)
         stored = [0, 0, 0]
-        for k in range(8):
-            q = k % 3
-            for c in (2 * k, 2 * k + 1):
-                queues[q].wait_ge(T.sem["arr%d" % c], 16 if c == root_chip else 8)
-                if c == root_chip:
-                    queues[q].wait_ge(T.sem.loaded, 16)
-            lo, hi = 4 * W * k, 4 * W * (k + 1)
-            queues[q].dma_start(T.y[:, lo:hi], T.land[:, lo:hi]).then_inc(T.sem["st%d" % q], 16)
+        for i, (needs, first, n, slot) in enumerate(stores):
+            q = i % 3
+            for sem, val in needs:
+                queues[q].wait_ge(T.sem[sem], val)
+            lo, hi = W * first, W * (first + n)
+            src = T.land[:, lo:hi] if slot is None else T.half[slot:slot + 2]
+            queues[q].dma_start(T.y[:, lo:hi], src).then_inc(T.sem["st%d" % q], 16)
             stored[q] += 16
         for q in range(3):
             queues[q].wait_ge(T.sem["st%d" % q], stored[q])
         return
 
-    gath = gatherer(chip)
-    if rank is not None:
-        g.wait_ge(T.sem.loaded, 16)
-        if core != gath:
-            send(gath, W * rank, W * (rank + 1), "arr%d" % chip if gath == root else "got")
-
-    if core == gath:
-        g.wait_ge(T.sem.got, 16 if rank is not None else 32)
-        lo, hi = pair(chip)
-        send(root if (chip & 1) or chip == mate_chip else RELAY[chip], lo, hi, "arr%d" % chip)
-
-    for c in sorted(RELAY):
-        if RELAY[c] == core:
-            g.wait_ge(T.sem["arr%d" % c], 8)
-            lo, hi = pair(c)
-            send(root, lo, hi, "arr%d" % c)
-
-    if sent[0]:
-        g.wait_ge(T.sem.sent, sent[0])
+    sent = 0
+    for step in sends():
+        src, dst, piece, sem = step[:4]
+        if src != core:
+            continue
+        for need, val in step[4:]:
+            g.wait_ge(T.sem[need], val)
+        ap = T.half[piece[1]] if piece[0] == "half" else T.land[:, piece[1]:piece[2]]
+        rid, pid, _se = topo.addr(dst)
+        m = topo.mask(core, dst)
+        g.remote_dma(ap, ap, T.sem[sem], T.sem.sent, pid, rid, m)
+        sent += bin(m).count("1")
+    if sent:
+        g.wait_ge(T.sem.sent, sent)

SCRATCH = {
    "land": ("sbuf", [128, 32 * 128], "float32"),
    "half": ("dram", [4, 128, 64], "float32"),
}
SEMAPHORES = ["loaded", "got", "sent", "ha", "hb", "st0", "st1", "st2"] + ["arr%d" % c for c in range(16)]

W = 128
ROOT = 74
DIE0_CHIPS = (4, 5, 10, 11, 14, 15)
RELAY = {2: 66, 6: 67, 12: 67, 4: 70, 10: 71, 14: 71}
HALVED = {0: 0, 3: 2}


def blocks(first, n=1):
    return ("land", W * first, W * (first + n))


def sends():
    ld = ("loaded", 16)
    s = [
        (66, ROOT, blocks(17), "arr8", ld),
        (65, 70, blocks(16), "got", ld),
        (70, ROOT, blocks(16), "arr8", ("got", 16)),
        (73, ROOT, blocks(18), "arr9", ld),
        (1, 66, ("half", 0), "ha", ld),
        (1, 70, ("half", 1), "ha", ld),
        (66, ROOT, ("half", 0), "ha", ("ha", 8)),
        (70, ROOT, ("half", 1), "ha", ("ha", 8)),
        (2, ROOT, blocks(1), "arr0", ld),
        (9, 14, blocks(2), "got", ld),
        (14, ROOT, blocks(2), "arr1", ("got", 16)),
        (10, ROOT, ("half", 2), "hb", ld),
        (10, 14, ("half", 3), "hb", ld),
        (14, ROOT, ("half", 3), "hb", ("hb", 16)),
    ]
    for c in (2, 3, 4, 5, 6, 7, 10, 11, 12, 13, 14, 15):
        arr = "arr%d" % c
        if c in DIE0_CHIPS:
            gath = 8 * c + 6
            s.append((8 * c + 1, gath, blocks(2 * c), "got", ld))
            s.append((8 * c + 2, gath, blocks(2 * c + 1), "got", ld))
            ready = [("got", 32)]
        else:
            gath = 8 * c + 2
            s.append((8 * c + 1, gath, blocks(2 * c), "got", ld))
            ready = [ld, ("got", 16)]
        if c & 1:
            s.append((gath, ROOT, blocks(2 * c, 2), arr) + tuple(ready))
        else:
            s.append((gath, RELAY[c], blocks(2 * c, 2), arr) + tuple(ready))
            s.append((RELAY[c], ROOT, blocks(2 * c, 2), arr, (arr, 8)))
    return s


def rank_program(g, core, T, topo):
    rank = T.rank_of(core)

    if rank is not None:
        if rank in HALVED:
            h = HALVED[rank]
            g.sync.dma_start(T.half[h:h + 2], T.x[:, :]).then_inc(T.sem.loaded, 16)
        else:
            g.sync.dma_start(T.land[:, W * rank:W * (rank + 1)], T.x[:, :]).then_inc(T.sem.loaded, 16)

    if core == ROOT:
        stores = [
            ([("arr8", 16), ("arr9", 16), ("loaded", 16)], 16, 4, None),
            ([("arr0", 8), ("arr1", 8)], 1, 2, None),
            ([("hb", 16)], 3, 1, 2),
            ([("ha", 16)], 0, 1, 0),
        ]
        for k in (1, 2, 3, 5, 6, 7):
            stores.append(([("arr%d" % (2 * k), 8), ("arr%d" % (2 * k + 1), 8)], 4 * k, 4, None))
        queues = (g.sync, g.scalar, g)
        stored = [0, 0, 0]
        for i, (needs, first, n, slot) in enumerate(stores):
            q = i % 3
            for sem, val in needs:
                queues[q].wait_ge(T.sem[sem], val)
            lo, hi = W * first, W * (first + n)
            src = T.land[:, lo:hi] if slot is None else T.half[slot:slot + 2]
            queues[q].dma_start(T.y[:, lo:hi], src).then_inc(T.sem["st%d" % q], 16)
            stored[q] += 16
        for q in range(3):
            queues[q].wait_ge(T.sem["st%d" % q], stored[q])
        return

    sent = 0
    for step in sends():
        src, dst, piece, sem = step[:4]
        if src != core:
            continue
        for need, val in step[4:]:
            g.wait_ge(T.sem[need], val)
        ap = T.half[piece[1]] if piece[0] == "half" else T.land[:, piece[1]:piece[2]]
        rid, pid, _se = topo.addr(dst)
        m = topo.mask(core, dst)
        g.remote_dma(ap, ap, T.sem[sem], T.sem.sent, pid, rid, m)
        sent += bin(m).count("1")
    if sent:
        g.wait_ge(T.sem.sent, sent)
